import numpy as np
import ml_dtypes


def mxq(x, axis, fmt="e4m3"):
    dtype, down = {"e4m3": (ml_dtypes.float8_e4m3fn, 7), "e5m2": (ml_dtypes.float8_e5m2, 14)}[fmt]
    v = np.moveaxis(np.asarray(x, np.float32).astype(ml_dtypes.bfloat16).astype(np.float64), axis, -1)
    blocks = v.reshape(v.shape[:-1] + (-1, 32))
    amax = np.abs(blocks).max(-1, keepdims=True)
    byte = np.maximum(np.where(amax > 0, np.frexp(amax)[1] - 1 + 127, 0) - down, 1)
    scale = np.exp2(byte - 127.0)
    codes = (blocks / scale).astype(np.float32).astype(dtype).astype(np.float64)
    return np.moveaxis((codes * scale).reshape(v.shape), -1, axis)


WIDE = False


def mx_kscale(k):
    if not WIDE:
        return np.ones(k)
    levels = np.array([10, -10, 5, -5, 0])
    if k % 512:
        return np.exp2(np.random.permutation(np.resize(levels, k // 32))).repeat(32)
    a = np.empty((k // 512, 16))
    for p in range(k // 512):
        a[p, :8] = np.random.permutation(np.resize(levels, 8))
        for g in range(8):
            far = levels[np.abs(levels - a[p, g]) >= 10]
            a[p, g + 8] = far[np.random.randint(len(far))]
    return np.exp2(a.ravel()).repeat(32)


def f64(x):
    return np.asarray(x).astype(np.float64)


def striped(idx):
    return np.tile(idx.reshape(-1, 16).T, (8, 1)).astype(np.uint16)


def unstriped(offs):
    return offs[:16].T.reshape(-1).astype(np.int64)


E2M1 = np.array([0.0, 0.5, 1.0, 1.5, 2.0, 3.0, 4.0, 6.0, -0.0, -0.5, -1.0, -1.5, -2.0, -3.0, -4.0, -6.0])


def pack_weight(w, fmt):
    k, n = w.shape
    w = f64(np.asarray(w, np.float32).astype(ml_dtypes.bfloat16)).reshape(k // 32, 32, n)
    amax = np.abs(w).max(1)
    if fmt == "e4m3":
        byte = np.frexp(amax)[1] - 1 + 127 - 7
    else:
        mant, ex = np.frexp(amax / 6.0)
        byte = np.where(mant > 0.5, ex, ex - 1) + 127
    byte = np.clip(np.where(amax > 0, byte, 1), 1, 254)
    scaled = (w * np.exp2(127.0 - byte)[:, None, :]).reshape(k, n).astype(np.float32)
    by_word = np.ascontiguousarray(scaled.reshape(k // 512, 128, 4, n).transpose(0, 1, 3, 2))
    if fmt == "e4m3":
        words = by_word.astype(ml_dtypes.float8_e4m3fn).view(np.uint8)
    else:
        c = by_word.astype(ml_dtypes.float4_e2m1fn).view(np.uint8) & 0xF
        words = (c[..., 0::2] | (c[..., 1::2] << 4)).reshape(k // 512, 128, 2 * n)
    return np.ascontiguousarray(words), np.ascontiguousarray(byte.astype(np.uint8).reshape(k // 512, 16, n))


def unpack_weight(words, scales, fmt):
    g, _, n = scales.shape
    words = np.ascontiguousarray(words).reshape(g, 128, n, -1)
    if fmt == "e4m3":
        vals = words.view(ml_dtypes.float8_e4m3fn).astype(np.float64)
    else:
        nib = np.empty((g, 128, n, 4), np.uint8)
        nib[..., 0::2] = words & 0xF
        nib[..., 1::2] = words >> 4
        vals = E2M1[nib]
    vals = vals * np.repeat(np.exp2(scales.astype(np.float64) - 127.0), 8, axis=1)[..., None]
    return vals.transpose(0, 1, 3, 2).reshape(g * 512, n)


def planes(y):
    n, m = y.shape
    v = y.astype(np.float32).astype(ml_dtypes.bfloat16).astype(np.float64).reshape(n // 32, 32, m)
    top = np.abs(v).max(1)
    byte = np.clip(np.where(top > 0, np.frexp(top)[1] - 1 + 127 - 7, 1), 1, 254)
    codes = (v * np.exp2(127.0 - byte)[:, None, :]).reshape(n, m).astype(np.float32).astype(ml_dtypes.float8_e4m3fn).view(np.uint8)
    words = codes.reshape(n // 512, 128, 4, m).transpose(0, 1, 3, 2)
    return np.ascontiguousarray(words), np.ascontiguousarray(byte.astype(np.uint8).reshape(n // 512, 16, m))


def relu(v):
    return np.maximum(v, 0.0)


K, T, E, C, H, N, HOT = 512, 640, 15, 128, 512, 512, 2
TOP = 3


def by_expert(wq, xq):
    return np.concatenate([wq[e].T @ xq[:, e * C:(e + 1) * C] for e in range(E)], axis=1)


def setup_inputs():
    n = np.random.standard_normal
    s = mx_kscale(K)
    u = mx_kscale(H)
    deal = np.repeat(np.arange(E), C).reshape(TOP, T)[:, np.random.permutation(T)]
    deal = np.take_along_axis(deal, np.argsort(np.random.rand(TOP, T), axis=0), axis=0)
    for _ in range(8):
        s_, t_ = np.random.permutation(T).reshape(2, -1); r = np.random.randint(TOP, size=T // 2); x, y = deal[r, s_].copy(), deal[r, t_].copy()
        ok = ~((deal[:, s_] == y).any(0) | (deal[:, t_] == x).any(0)); deal[r[ok], s_[ok]] = y[ok]; deal[r[ok], t_[ok]] = x[ok]
    order = np.lexsort((np.random.rand(TOP * T), deal.reshape(-1)))
    slot_token = order % T; pos = np.empty(TOP * T, np.int64); pos[order] = np.arange(TOP * T); pos = pos.reshape(TOP, T)
    g = np.random.uniform(0.5, 1.5, (TOP, T)); g = g / g.sum(0)
    x = pack_weight(n((K, T)) * s[:, None], "e4m3")
    w1h = [pack_weight(m, "e4m3") for m in n((HOT, K, H)) / np.sqrt(K) / s[None, :, None] * u]
    w2h = [pack_weight(m, "e4m3") for m in n((HOT, H, N)) / np.sqrt(H) / u[None, :, None]]
    w1c = [pack_weight(m, "e2m1") for m in n((E - HOT, K, H)) / np.sqrt(K) / s[None, :, None] * u]
    w2c = [pack_weight(m, "e2m1") for m in n((E - HOT, H, N)) / np.sqrt(H) / u[None, :, None]]
    return {
        "x_words": x[0],
        "x_scales": x[1],
        "w1h_words": np.stack([m[0] for m in w1h]),
        "w1h_scales": np.stack([m[1] for m in w1h]),
        "w2h_words": np.stack([m[0] for m in w2h]),
        "w2h_scales": np.stack([m[1] for m in w2h]),
        "w1c_words": np.stack([m[0] for m in w1c]),
        "w1c_scales": np.stack([m[1] for m in w1c]),
        "w2c_words": np.stack([m[0] for m in w2c]),
        "w2c_scales": np.stack([m[1] for m in w2c]),
        "gate": np.stack([np.tile(r, (128, 1)) for r in g]).astype(np.float32),
        "offs": striped(slot_token),
        "pos1": striped(pos[0]),
        "pos2": striped(pos[1]),
        "pos3": striped(pos[2]),
    }


def reference(x_words, x_scales, w1h_words, w1h_scales, w2h_words, w2h_scales, w1c_words, w1c_scales, w2c_words, w2c_scales, gate, offs, pos1, pos2, pos3):
    w1h = np.stack([unpack_weight(w1h_words[e], w1h_scales[e], "e4m3") for e in range(HOT)])
    w2h = np.stack([unpack_weight(w2h_words[e], w2h_scales[e], "e4m3") for e in range(HOT)])
    w1c = np.stack([unpack_weight(w1c_words[e], w1c_scales[e], "e2m1") for e in range(E - HOT)])
    w2c = np.stack([unpack_weight(w2c_words[e], w2c_scales[e], "e2m1") for e in range(E - HOT)])
    idx = unstriped(offs)
    xq = unpack_weight(x_words, x_scales, "e4m3")[:, idx]
    w1 = [*w1h, *w1c]
    w2 = [*w2h, *w2c]
    h = relu(by_expert(w1, xq))
    y = by_expert(w2, mxq(h, 0, "e4m3"))
    out = sum(f64(gate[r, :1]) * y[:, unstriped(p)] for r, p in enumerate((pos1, pos2, pos3)))
    out_0 = out
    return (out_0,) + planes(out_0)

@@ -1,0 +1,268 @@
+from contextlib import ExitStack
+
+import concourse.mybir as mybir
+from concourse.masks import make_identity
+
+K, T, E, C, H, N, HOT, TOP = 512, 640, 15, 128, 512, 512, 2, 3
+S = E * C
+P = 128
+FLOPS = 2 * S * (K * H + H * N)
+
+F32 = mybir.dt.float32
+BF16 = mybir.dt.bfloat16
+I32 = mybir.dt.int32
+U32 = mybir.dt.uint32
+U16 = mybir.dt.uint16
+U8 = mybir.dt.uint8
+FP8X4 = mybir.dt.float8_e4m3fn_x4
+FP4X4 = mybir.dt.float4_e2m1fn_x4
+RELU = mybir.ActivationFunctionType.Relu
+MULT = mybir.AluOpType.mult
+
+GATHER_EXPERTS = [1, 2, 3, 3, 3, 3]
+GROUP_EXPERTS = [1, 2, 2, 2, 2, 2, 2, 1, 1]
+W1_WORD_LOADS = [(0, 1), (1, 2), (2, 5), (5, 9), (9, 15)]
+W1_SCALE_LOADS = [(0, 2), (2, 15)]
+W2_WORD_LOADS = [(0, 2), (2, 9), (9, 15)]
+W2_SCALE_LOADS = [(0, 2), (2, 15)]
+Y_BANK_EXPERTS = [(0, 4), (4, 8), (8, 12), (12, 15)]
+TOKEN_CHUNKS = [(0, 3), (3, 4), (4, 5)]
+VECTOR_WORD_GROUPS = (3, 5, 6, 7, 8)
+Y_BANK = [[6, 7, 3, 0], [1, 2, 4, 5]]
+SUM_BANK = [6, 7, 3, 4, 5]
+BACK_BANK = [0, 1, 2, 6, 7]
+GATE_LOADS = [(0, 3), (3, 5)]
+
+
+def runs(sizes):
+    out, at = [], 0
+    for n in sizes:
+        out.append((at, at + n))
+        at += n
+    return out
+
+
+def tile_moe_hot_mlp_relu_kernel(
+    tc, x_words, x_scales, w1h_words, w1h_scales, w2h_words, w2h_scales,
+    w1c_words, w1c_scales, w2c_words, w2c_scales, gate, offs, pos1, pos2, pos3,
+    out_0, out_1, out_2,
+):
+    nc = tc.nc
+    with ExitStack() as ctx:
+        keep = ctx.enter_context(tc.tile_pool(name="keep", bufs=1))
+        work = ctx.enter_context(tc.tile_pool(name="work", bufs=3))
+        psum = ctx.enter_context(tc.psum_pool(name="psum", bufs=1))
+        banks = [psum.tile([P, 512], F32, name="bank%d" % i) for i in range(8)]
+
+        offs_t = keep.tile([P, S // 16], U16, name="offs_t")
+        pos_t = [keep.tile([P, T // 16], U16, name="pos_t%d" % r) for r in range(TOP)]
+        xw = keep.tile([P, T], I32, name="xw", align_bytes=64)
+        xs = keep.tile([P, T], U8, name="xs", align_bytes=64)
+
+        def scale_tile(name, lo, hi):
+            t = keep.tile([P, hi - lo, 512], U8, name="%s_%d" % (name, lo), align_bytes=64)
+            eng = nc.vector if name == "s1" and lo >= HOT else nc.gpsimd
+            eng.memset(t[:].rearrange("p e n -> p (e n)").bitcast(I32), 0)
+            return t
+
+        def load_scales(t, hot, cold, lo, hi):
+            first = lo if lo < HOT else lo - HOT
+            src = (hot if lo < HOT else cold).rearrange("e s b n -> (e s) b n").bitcast(I32)
+            rows = src[first : first + hi - lo].rearrange("e (q r) w -> r q e w", r=4)
+            for r in range(4):
+                nc.sync.dma_start(out=t[r:P:32].bitcast(I32), in_=rows[r])
+
+        def load_words(name, hot, cold, lo, hi):
+            if lo < HOT:
+                src = hot.rearrange("e s p n d -> (e s) p (n d)").bitcast(I32)[lo:hi]
+            else:
+                src = cold.rearrange("e s p b -> (e s) p b").bitcast(I32)[lo - HOT : hi - HOT]
+            shape = [P, hi - lo, 4 * src.shape[2]]
+            t = keep.tile(shape, U8, name="%s_%d" % (name, lo), align_bytes=64)
+            nc.sync.dma_start(out=t[:].bitcast(I32), in_=src.rearrange("e p w -> p e w"))
+            return t
+
+        nc.gpsimd.memset(xs[:].bitcast(I32), 0)
+        warm = keep.tile([P, 16], F32, name="warm")
+        nc.vector.memset(warm[:, 0:1], 0.0)
+        s1 = {lo: scale_tile("s1", lo, hi) for lo, hi in W1_SCALE_LOADS}
+        ident = keep.tile([P, P], F32, name="ident", align_bytes=64)
+        make_identity(nc, ident[:])
+        s2 = {lo: scale_tile("s2", lo, hi) for lo, hi in W2_SCALE_LOADS}
+
+        nc.scalar.activation(warm[:, 8:9], warm[:, 0:1], RELU)
+        nc.sync.dma_start(offs_t[:], offs)
+        x_rows = x_scales[0].rearrange("(q r) t -> r q t", r=4)
+        for r in range(4):
+            nc.sync.dma_start(out=xs[r:P:32].bitcast(I32), in_=x_rows[r].bitcast(I32))
+        nc.sync.dma_start(out=xw[:], in_=x_words[0].rearrange("p t d -> p (t d)").bitcast(I32))
+        w1 = {}
+        w2 = {}
+        for lo, hi in W1_WORD_LOADS[:2]:
+            w1[lo] = load_words("w1", w1h_words, w1c_words, lo, hi)
+        load_scales(s1[0], w1h_scales, w1c_scales, *W1_SCALE_LOADS[0])
+        w1[2] = load_words("w1", w1h_words, w1c_words, *W1_WORD_LOADS[2])
+        load_scales(s1[2], w1h_scales, w1c_scales, *W1_SCALE_LOADS[1])
+        for lo, hi in W1_WORD_LOADS[3:]:
+            w1[lo] = load_words("w1", w1h_words, w1c_words, lo, hi)
+        for lo, hi in W2_WORD_LOADS:
+            w2[lo] = load_words("w2", w2h_words, w2c_words, lo, hi)
+        for r, src in enumerate((pos1, pos2, pos3)):
+            nc.sync.dma_start(pos_t[r][:], src)
+        gate_t = []
+        for b0, b1 in GATE_LOADS:
+            g = keep.tile([P, TOP, (b1 - b0) * P], F32, name="gate_t%d" % b0)
+            nc.sync.dma_start(out=g[:], in_=gate.rearrange("r p t -> p r t")[:, :, b0 * P : b1 * P])
+            gate_t.append(g)
+            if b0 == 0:
+                for lo, hi in W2_SCALE_LOADS:
+                    load_scales(s2[lo], w2h_scales, w2c_scales, lo, hi)
+
+        def held(tiles, loads, e):
+            lo = [a for a, b in loads if a <= e < b][0]
+            return tiles[lo][:, e - lo, :]
+
+        def codes(words, e, c0, c1):
+            if e < HOT:
+                return words[:, 4 * c0 : 4 * c1].bitcast(FP8X4)
+            return words[:, 2 * c0 : 2 * c1].bitcast(FP4X4)
+
+        gathered = {}
+
+        widest = max(GATHER_EXPERTS) * C
+        gw_ring = [keep.tile([P, widest], U32, name="gw%d" % i, align_bytes=64) for i in range(2)]
+        gs_ring = [keep.tile([P, widest], U8, name="gs%d" % i, align_bytes=64) for i in range(2)]
+
+        def gather_tokens(i, lo, hi):
+            n = (hi - lo) * C
+            lst = offs_t[:, lo * C // 16 : hi * C // 16]
+            gw = gw_ring[i % 2][:, 0:n]
+            gs = gs_ring[i % 2][:, 0:n]
+            nc.vector.tensor_copy(gw, xw[:].bitcast(U32).indirect(lst))
+            nc.vector.tensor_copy(gs, xs[:].indirect(lst))
+            for e in range(lo, hi):
+                cols = slice((e - lo) * C, (e - lo + 1) * C)
+                gathered[e] = (gw[:, cols], gs[:, cols])
+
+        sorted_h = {}
+
+        def first_product(e, bank):
+            gw, gs = gathered[e]
+            nc.tensor.matmul_mx(
+                out=bank[:], lhsT=gw.bitcast(FP8X4), lhsT_scale=gs,
+                rhs=codes(held(w1, W1_WORD_LOADS, e), e, 0, H), rhs_scale=held(s1, W1_SCALE_LOADS, e),
+                start=True, stop=True,
+            )
+            hs = work.tile([P, H], BF16, name="hs", bufs=5, align_bytes=64)
+            nc.scalar.activation(
+                hs[:].rearrange("s (u m v) -> s u m v", u=2, v=2),
+                bank[:].rearrange("s (m u v) -> s u m v", u=2, v=2), RELU,
+            )
+            sorted_h[e] = hs
+
+        hq = {}
+
+        def turn_and_quantise(g, lo, hi):
+            n = hi - lo
+            bank = banks[4 + g % 2][:, 0 : n * 2 * C].rearrange("p (e u s) -> p e u s", e=n, u=2)
+            for e in range(lo, hi):
+                words = sorted_h[e][:].bitcast(F32)
+                for u in range(2):
+                    nc.tensor.transpose(bank[:, e - lo, u, :], words[:, u * P : (u + 1) * P], ident[:])
+            hb = work.tile([P, n * C * 4], BF16, name="hb", align_bytes=64)
+            dst = hb[:].bitcast(F32).rearrange("p (e s u) -> p e s u", e=n, u=2)
+            src = bank.rearrange("p e u s -> p e s u")
+            if g in VECTOR_WORD_GROUPS:
+                nc.vector.tensor_copy(dst, src)
+            else:
+                nc.scalar.copy(dst, src)
+            qw = keep.tile([P, n * C], U32, name="qw%d" % lo, align_bytes=64)
+            qs = keep.tile([P, n * C], U8, name="qs%d" % lo, align_bytes=64)
+            nc.vector.quantize_mx(out=qw[:].bitcast(FP8X4), scales=qs[:], in_=hb[:])
+            for e in range(lo, hi):
+                cols = slice((e - lo) * C, (e - lo + 1) * C)
+                hq[e] = (qw[:, cols], qs[:, cols])
+
+        y = [keep.tile([P, S], F32, name="y%d" % t) for t in range(4)]
+
+        def second_product(t, i, on_vector=False):
+            lo, hi = Y_BANK_EXPERTS[i]
+            bank = banks[Y_BANK[t % 2][i]]
+            for e in range(lo, hi):
+                qw, qs = hq[e]
+                nc.tensor.matmul_mx(
+                    out=bank[:, (e - lo) * C : (e - lo + 1) * C],
+                    lhsT=codes(held(w2, W2_WORD_LOADS, e), e, t * P, (t + 1) * P),
+                    lhsT_scale=held(s2, W2_SCALE_LOADS, e)[:, t * P : (t + 1) * P],
+                    rhs=qw.bitcast(FP8X4), rhs_scale=qs, start=True, stop=True,
+                )
+            copy = nc.vector.tensor_copy if on_vector else nc.scalar.copy
+            copy(y[t][:, lo * C : hi * C], bank[:, 0 : (hi - lo) * C])
+
+        groups = runs(GROUP_EXPERTS)
+        gathers = runs(GATHER_EXPERTS)
+        for step in range(len(groups) + 1):
+            if step < len(gathers):
+                gather_tokens(step, *gathers[step])
+            if step < len(groups):
+                for e in range(*groups[step]):
+                    first_product(e, banks[e % 4])
+            if step >= 1:
+                turn_and_quantise(step - 1, *groups[step - 1])
+        for t in range(4):
+            for i in range(len(Y_BANK_EXPERTS)):
+                second_product(t, i, on_vector=(t == 0 and i % 2 == 1))
+
+        ow = keep.tile([P, T], U32, name="ow", align_bytes=64)
+        osc = keep.tile([P, T], U8, name="osc", align_bytes=64)
+        out_rows = out_0.rearrange("(p j) t -> p j t", j=4)
+        out_words = out_1[0].rearrange("p t d -> p (t d)").bitcast(I32)
+        out_sc = out_2[0].rearrange("(q r) t -> r q t", r=4)
+        widest = max(b1 - b0 for b0, b1 in TOKEN_CHUNKS) * P
+        looked_up = [
+            [keep.tile([P, widest], F32, name="g%d_%d" % (t, r)) for r in range(TOP)] for t in range(4)
+        ]
+        for ci, (b0, b1) in enumerate(TOKEN_CHUNKS):
+            nb = b1 - b0
+            last = ci == len(TOKEN_CHUNKS) - 1
+            tok = slice(b0 * P, b1 * P)
+            gi = [i for i, (a, b) in enumerate(GATE_LOADS) if a <= b0 < b][0]
+            g0 = (b0 - GATE_LOADS[gi][0]) * P
+            sums = [banks[SUM_BANK[b0 + b]][:].rearrange("k (t n) -> k t n", t=4) for b in range(nb)]
+            turned = [keep.tile([P, 4, 4, 32], F32, name="turned%d" % (b0 + b)) for b in range(nb)]
+            for t in range(4):
+                parts = []
+                for r in range(TOP):
+                    g = looked_up[t][r][:, 0 : nb * P]
+                    nc.vector.tensor_tensor(
+                        g, y[t][:].indirect(pos_t[r][:, b0 * 8 : b1 * 8]),
+                        gate_t[gi][:, r, g0 : g0 + nb * P], MULT,
+                    )
+                    parts.append(g)
+                for b in range(nb):
+                    for r in range(TOP):
+                        nc.tensor.matmul(
+                            sums[b][:, t, :], parts[r][:, b * P : (b + 1) * P], ident[:],
+                            start=(r == 0), stop=(r == TOP - 1), is_transpose=True,
+                        )
+                if last:
+                    nc.scalar.copy(turned[0][:, :, t, :], sums[0][:, t, :].rearrange("k (m j) -> k j m", j=4))
+            o32 = keep.tile([P, 4, nb * P], F32, name="o32_%d" % ci)
+            if not last:
+                for b in range(nb):
+                    nc.scalar.copy(turned[b][:], sums[b].rearrange("k t (m j) -> k j t m", j=4))
+            for b in range(nb):
+                back = banks[BACK_BANK[b0 + b]][:].rearrange("p (j k) -> p j k", j=4)
+                for j in range(4):
+                    nc.tensor.transpose(back[:, j, :], turned[b][:, j].rearrange("k t m -> k (t m)"), ident[:])
+                ob = keep.tile([P, P * 4], BF16, name="ob%d" % (b0 + b), align_bytes=64)
+                copy = nc.vector.tensor_copy if last else nc.scalar.copy
+                copy(ob[:].rearrange("p (k j) -> p k j", j=4), back.rearrange("p j k -> p k j"))
+                nc.scalar.copy(o32[:, :, b * P : (b + 1) * P], back)
+                cols = slice((b0 + b) * P, (b0 + b + 1) * P)
+                nc.vector.quantize_mx(out=ow[:, cols].bitcast(FP8X4), scales=osc[:, cols], in_=ob[:])
+            store = nc.scalar if last else nc.sync
+            store.dma_start(out=out_rows[:, :, tok], in_=o32[:])
+            nc.sync.dma_start(out=out_words[:, tok], in_=ow[:, tok].bitcast(I32))
+        for r in range(4):
+            nc.sync.dma_start(out=out_sc[r].bitcast(I32), in_=osc[r:P:32].bitcast(I32))

@@ -19,27 +19,19 @@ FP4X4 = mybir.dt.float4_e2m1fn_x4
 RELU = mybir.ActivationFunctionType.Relu
 MULT = mybir.AluOpType.mult
 
-GATHER_EXPERTS = [1, 2, 3, 3, 3, 3]
-GROUP_EXPERTS = [1, 2, 2, 2, 2, 2, 2, 1, 1]
-W1_WORD_LOADS = [(0, 1), (1, 2), (2, 5), (5, 9), (9, 15)]
-W1_SCALE_LOADS = [(0, 2), (2, 15)]
-W2_WORD_LOADS = [(0, 2), (2, 9), (9, 15)]
-W2_SCALE_LOADS = [(0, 2), (2, 15)]
-Y_BANK_EXPERTS = [(0, 4), (4, 8), (8, 12), (12, 15)]
-TOKEN_CHUNKS = [(0, 3), (3, 4), (4, 5)]
-VECTOR_WORD_GROUPS = (3, 5, 6, 7, 8)
+GATHERS = [(14, 15), (13, 14), (11, 13), (8, 11), (5, 8), (2, 5), (0, 2)]
+GROUPS = [(14, 15), (12, 14), (10, 12), (8, 10), (6, 8), (4, 6), (2, 4), (1, 2), (0, 1)]
+W1_WORD_LOADS = [(13, 15), (9, 13), (2, 9), (0, 2)]
+W1_SCALE_LOADS = [(11, 15), (2, 11), (0, 2)]
+W2_WORD_LOADS = [(9, 15), (2, 9), (0, 2)]
+Y_BANK_EXPERTS = [(11, 15), (7, 11), (3, 7), (0, 3)]
+TOKEN_CHUNKS = [(0, 2), (2, 3), (3, 4), (4, 5)]
+VECTOR_WORD_GROUPS = (6, 7, 8)
 Y_BANK = [[6, 7, 3, 0], [1, 2, 4, 5]]
-SUM_BANK = [6, 7, 3, 4, 5]
-BACK_BANK = [0, 1, 2, 6, 7]
+SUM_BANK = [6, 7, 3, 3, 3]
+BACK_BANK = [0, 1, 2, 4, 5]
+SORT_CUTS = [[0, 2, 4], [0, 4], [0, 4], [0, 3, 4]]
 GATE_LOADS = [(0, 3), (3, 5)]
-
-
-def runs(sizes):
-    out, at = [], 0
-    for n in sizes:
-        out.append((at, at + n))
-        at += n
-    return out
 
 
 def tile_moe_hot_mlp_relu_kernel(
@@ -59,16 +51,16 @@ def tile_moe_hot_mlp_relu_kernel(
         xw = keep.tile([P, T], I32, name="xw", align_bytes=64)
         xs = keep.tile([P, T], U8, name="xs", align_bytes=64)
 
-        def scale_tile(name, lo, hi):
-            t = keep.tile([P, hi - lo, 512], U8, name="%s_%d" % (name, lo), align_bytes=64)
-            eng = nc.vector if name == "s1" and lo >= HOT else nc.gpsimd
-            eng.memset(t[:].rearrange("p e n -> p (e n)").bitcast(I32), 0)
+        def scale_tile(name, lo, hi, width):
+            t = keep.tile([P, hi - lo, width], U8, name="%s_%d" % (name, lo), align_bytes=64)
+            engine = nc.vector if name == "s1" else nc.gpsimd
+            engine.memset(t[:].rearrange("p e n -> p (e n)").bitcast(I32), 0)
             return t
 
-        def load_scales(t, hot, cold, lo, hi):
+        def load_scales(t, hot, cold, lo, hi, c0, c1):
             first = lo if lo < HOT else lo - HOT
             src = (hot if lo < HOT else cold).rearrange("e s b n -> (e s) b n").bitcast(I32)
-            rows = src[first : first + hi - lo].rearrange("e (q r) w -> r q e w", r=4)
+            rows = src[first : first + hi - lo, :, c0 // 4 : c1 // 4].rearrange("e (q r) w -> r q e w", r=4)
             for r in range(4):
                 nc.sync.dma_start(out=t[r:P:32].bitcast(I32), in_=rows[r])
 
@@ -85,10 +77,11 @@ def tile_moe_hot_mlp_relu_kernel(
         nc.gpsimd.memset(xs[:].bitcast(I32), 0)
         warm = keep.tile([P, 16], F32, name="warm")
         nc.vector.memset(warm[:, 0:1], 0.0)
-        s1 = {lo: scale_tile("s1", lo, hi) for lo, hi in W1_SCALE_LOADS}
+        s1 = {lo: scale_tile("s1", lo, hi, H) for lo, hi in W1_SCALE_LOADS}
         ident = keep.tile([P, P], F32, name="ident", align_bytes=64)
         make_identity(nc, ident[:])
-        s2 = {lo: scale_tile("s2", lo, hi) for lo, hi in W2_SCALE_LOADS}
+        s2_hot = scale_tile("s2h", 0, HOT, N)
+        s2_cold = [scale_tile("s2c%d" % a, HOT, E, N // 2) for a in range(2)]
 
         nc.scalar.activation(warm[:, 8:9], warm[:, 0:1], RELU)
         nc.sync.dma_start(offs_t[:], offs)
@@ -98,25 +91,30 @@ def tile_moe_hot_mlp_relu_kernel(
         nc.sync.dma_start(out=xw[:], in_=x_words[0].rearrange("p t d -> p (t d)").bitcast(I32))
         w1 = {}
         w2 = {}
-        for lo, hi in W1_WORD_LOADS[:2]:
+        for i in range(2):
+            w1[W1_WORD_LOADS[i][0]] = load_words("w1", w1h_words, w1c_words, *W1_WORD_LOADS[i])
+            lo, hi = W1_SCALE_LOADS[i]
+            load_scales(s1[lo], w1h_scales, w1c_scales, lo, hi, 0, H)
+        for lo, hi in W1_WORD_LOADS[2:]:
             w1[lo] = load_words("w1", w1h_words, w1c_words, lo, hi)
-        load_scales(s1[0], w1h_scales, w1c_scales, *W1_SCALE_LOADS[0])
-        w1[2] = load_words("w1", w1h_words, w1c_words, *W1_WORD_LOADS[2])
-        load_scales(s1[2], w1h_scales, w1c_scales, *W1_SCALE_LOADS[1])
-        for lo, hi in W1_WORD_LOADS[3:]:
-            w1[lo] = load_words("w1", w1h_words, w1c_words, lo, hi)
-        for lo, hi in W2_WORD_LOADS:
-            w2[lo] = load_words("w2", w2h_words, w2c_words, lo, hi)
+        w2[9] = load_words("w2", w2h_words, w2c_words, *W2_WORD_LOADS[0])
+        load_scales(s1[0], w1h_scales, w1c_scales, 0, HOT, 0, H)
+        w2[2] = load_words("w2", w2h_words, w2c_words, *W2_WORD_LOADS[1])
+        load_scales(s2_hot, w2h_scales, w2c_scales, 0, HOT, 0, N)
+        w2[0] = load_words("w2", w2h_words, w2c_words, *W2_WORD_LOADS[2])
         for r, src in enumerate((pos1, pos2, pos3)):
             nc.sync.dma_start(pos_t[r][:], src)
         gate_t = []
-        for b0, b1 in GATE_LOADS:
+        for a, (b0, b1) in enumerate(GATE_LOADS):
+            load_scales(s2_cold[a], w2h_scales, w2c_scales, HOT, E, a * N // 2, (a + 1) * N // 2)
             g = keep.tile([P, TOP, (b1 - b0) * P], F32, name="gate_t%d" % b0)
             nc.sync.dma_start(out=g[:], in_=gate.rearrange("r p t -> p r t")[:, :, b0 * P : b1 * P])
             gate_t.append(g)
-            if b0 == 0:
-                for lo, hi in W2_SCALE_LOADS:
-                    load_scales(s2[lo], w2h_scales, w2c_scales, lo, hi)
+
+        def second_scales(e, t):
+            if e < HOT:
+                return s2_hot[:, e, t * P : (t + 1) * P]
+            return s2_cold[t // 2][:, e - HOT, t % 2 * P : (t % 2 + 1) * P]
 
         def held(tiles, loads, e):
             lo = [a for a, b in loads if a <= e < b][0]
@@ -129,15 +127,15 @@ def tile_moe_hot_mlp_relu_kernel(
 
         gathered = {}
 
-        widest = max(GATHER_EXPERTS) * C
-        gw_ring = [keep.tile([P, widest], U32, name="gw%d" % i, align_bytes=64) for i in range(2)]
-        gs_ring = [keep.tile([P, widest], U8, name="gs%d" % i, align_bytes=64) for i in range(2)]
+        widest = max(hi - lo for lo, hi in GATHERS) * C
+        gw_ring = [keep.tile([P, widest], U32, name="gw%d" % i, align_bytes=64) for i in range(3)]
+        gs_ring = [keep.tile([P, widest], U8, name="gs%d" % i, align_bytes=64) for i in range(3)]
 
         def gather_tokens(i, lo, hi):
             n = (hi - lo) * C
             lst = offs_t[:, lo * C // 16 : hi * C // 16]
-            gw = gw_ring[i % 2][:, 0:n]
-            gs = gs_ring[i % 2][:, 0:n]
+            gw = gw_ring[i % 3][:, 0:n]
+            gs = gs_ring[i % 3][:, 0:n]
             nc.vector.tensor_copy(gw, xw[:].bitcast(U32).indirect(lst))
             nc.vector.tensor_copy(gs, xs[:].indirect(lst))
             for e in range(lo, hi):
@@ -188,25 +186,26 @@ def tile_moe_hot_mlp_relu_kernel(
         def second_product(t, i, on_vector=False):
             lo, hi = Y_BANK_EXPERTS[i]
             bank = banks[Y_BANK[t % 2][i]]
-            for e in range(lo, hi):
+            for e in reversed(range(lo, hi)):
                 qw, qs = hq[e]
                 nc.tensor.matmul_mx(
                     out=bank[:, (e - lo) * C : (e - lo + 1) * C],
                     lhsT=codes(held(w2, W2_WORD_LOADS, e), e, t * P, (t + 1) * P),
-                    lhsT_scale=held(s2, W2_SCALE_LOADS, e)[:, t * P : (t + 1) * P],
+                    lhsT_scale=second_scales(e, t),
                     rhs=qw.bitcast(FP8X4), rhs_scale=qs, start=True, stop=True,
                 )
             copy = nc.vector.tensor_copy if on_vector else nc.scalar.copy
             copy(y[t][:, lo * C : hi * C], bank[:, 0 : (hi - lo) * C])
 
-        groups = runs(GROUP_EXPERTS)
-        gathers = runs(GATHER_EXPERTS)
+        groups = GROUPS
+        gathers = GATHERS
+        gather_tokens(0, *gathers[0])
         for step in range(len(groups) + 1):
-            if step < len(gathers):
-                gather_tokens(step, *gathers[step])
+            if step + 1 < len(gathers):
+                gather_tokens(step + 1, *gathers[step + 1])
             if step < len(groups):
-                for e in range(*groups[step]):
-                    first_product(e, banks[e % 4])
+                for e in reversed(range(*groups[step])):
+                    first_product(e, banks[(E - 1 - e) % 4])
             if step >= 1:
                 turn_and_quantise(step - 1, *groups[step - 1])
         for t in range(4):
@@ -218,51 +217,68 @@ def tile_moe_hot_mlp_relu_kernel(
         out_rows = out_0.rearrange("(p j) t -> p j t", j=4)
         out_words = out_1[0].rearrange("p t d -> p (t d)").bitcast(I32)
         out_sc = out_2[0].rearrange("(q r) t -> r q t", r=4)
-        widest = max(b1 - b0 for b0, b1 in TOKEN_CHUNKS) * P
-        looked_up = [
-            [keep.tile([P, widest], F32, name="g%d_%d" % (t, r)) for r in range(TOP)] for t in range(4)
-        ]
+        wide = [[keep.tile([P, 2 * P], F32, name="g%d_%d" % (t, r)) for r in range(TOP)] for t in range(4)]
+        spare = [keep.tile([P, P], F32, name="spare%d" % r) for r in range(TOP)]
+
+        def products(ci, t):
+            if ci == 0:
+                return [g[:] for g in wide[t]]
+            if (ci, t) == (1, 0):
+                return [g[:] for g in spare]
+            n = (t - 1) % 4
+            return [g[:, n % 2 * P : (n % 2 + 1) * P] for g in wide[2 + n // 2]]
+
+        def look_up(ci, t):
+            b0, b1 = TOKEN_CHUNKS[ci]
+            gi = [i for i, (a, b) in enumerate(GATE_LOADS) if a <= b0 < b][0]
+            g0 = GATE_LOADS[gi][0]
+            for r, g in enumerate(products(ci, t)):
+                nc.vector.tensor_tensor(
+                    g, y[t][:].indirect(pos_t[r][:, b0 * 8 : b1 * 8]),
+                    gate_t[gi][:, r, (b0 - g0) * P : (b1 - g0) * P], MULT,
+                )
+
         for ci, (b0, b1) in enumerate(TOKEN_CHUNKS):
             nb = b1 - b0
             last = ci == len(TOKEN_CHUNKS) - 1
             tok = slice(b0 * P, b1 * P)
-            gi = [i for i, (a, b) in enumerate(GATE_LOADS) if a <= b0 < b][0]
-            g0 = (b0 - GATE_LOADS[gi][0]) * P
             sums = [banks[SUM_BANK[b0 + b]][:].rearrange("k (t n) -> k t n", t=4) for b in range(nb)]
             turned = [keep.tile([P, 4, 4, 32], F32, name="turned%d" % (b0 + b)) for b in range(nb)]
+            cuts = SORT_CUTS[ci]
             for t in range(4):
-                parts = []
+                if (ci, t) != (1, 0):
+                    look_up(ci, t)
+                if (ci, t) == (0, 0):
+                    look_up(1, 0)
+                parts = products(ci, t)
                 for r in range(TOP):
-                    g = looked_up[t][r][:, 0 : nb * P]
-                    nc.vector.tensor_tensor(
-                        g, y[t][:].indirect(pos_t[r][:, b0 * 8 : b1 * 8]),
-                        gate_t[gi][:, r, g0 : g0 + nb * P], MULT,
-                    )
-                    parts.append(g)
-                for b in range(nb):
-                    for r in range(TOP):
+                    for b in range(nb):
                         nc.tensor.matmul(
                             sums[b][:, t, :], parts[r][:, b * P : (b + 1) * P], ident[:],
                             start=(r == 0), stop=(r == TOP - 1), is_transpose=True,
                         )
-                if last:
-                    nc.scalar.copy(turned[0][:, :, t, :], sums[0][:, t, :].rearrange("k (m j) -> k j m", j=4))
+                if t + 1 in cuts:
+                    done = slice(cuts[cuts.index(t + 1) - 1], t + 1)
+                    for b in range(nb):
+                        nc.scalar.copy(
+                            turned[b][:, :, done, :], sums[b][:, done, :].rearrange("k t (m j) -> k j t m", j=4)
+                        )
             o32 = keep.tile([P, 4, nb * P], F32, name="o32_%d" % ci)
-            if not last:
-                for b in range(nb):
-                    nc.scalar.copy(turned[b][:], sums[b].rearrange("k t (m j) -> k j t m", j=4))
             for b in range(nb):
                 back = banks[BACK_BANK[b0 + b]][:].rearrange("p (j k) -> p j k", j=4)
                 for j in range(4):
                     nc.tensor.transpose(back[:, j, :], turned[b][:, j].rearrange("k t m -> k (t m)"), ident[:])
                 ob = keep.tile([P, P * 4], BF16, name="ob%d" % (b0 + b), align_bytes=64)
-                copy = nc.vector.tensor_copy if last else nc.scalar.copy
-                copy(ob[:].rearrange("p (k j) -> p k j", j=4), back.rearrange("p j k -> p k j"))
                 nc.scalar.copy(o32[:, :, b * P : (b + 1) * P], back)
+                if last:
+                    nc.vector.tensor_copy(ob[:].rearrange("p (k j) -> p k j", j=4), o32[:].rearrange("p j k -> p k j"))
+                else:
+                    nc.scalar.copy(ob[:].rearrange("p (k j) -> p k j", j=4), back.rearrange("p j k -> p k j"))
                 cols = slice((b0 + b) * P, (b0 + b + 1) * P)
                 nc.vector.quantize_mx(out=ow[:, cols].bitcast(FP8X4), scales=osc[:, cols], in_=ob[:])
             store = nc.scalar if last else nc.sync
             store.dma_start(out=out_rows[:, :, tok], in_=o32[:])
             nc.sync.dma_start(out=out_words[:, tok], in_=ow[:, tok].bitcast(I32))
         for r in range(4):
-            nc.sync.dma_start(out=out_sc[r].bitcast(I32), in_=osc[r:P:32].bitcast(I32))
+            store = nc.sync if r < 2 else nc.scalar
+            store.dma_start(out=out_sc[r].bitcast(I32), in_=osc[r:P:32].bitcast(I32))

from contextlib import ExitStack

import concourse.mybir as mybir
from concourse.masks import make_identity

K, T, E, C, H, N, HOT, TOP = 512, 640, 15, 128, 512, 512, 2, 3
S = E * C
P = 128
FLOPS = 2 * S * (K * H + H * N)

F32 = mybir.dt.float32
BF16 = mybir.dt.bfloat16
I32 = mybir.dt.int32
U32 = mybir.dt.uint32
U16 = mybir.dt.uint16
U8 = mybir.dt.uint8
FP8X4 = mybir.dt.float8_e4m3fn_x4
FP4X4 = mybir.dt.float4_e2m1fn_x4
RELU = mybir.ActivationFunctionType.Relu
MULT = mybir.AluOpType.mult

GATHERS = [(14, 15), (13, 14), (11, 13), (8, 11), (5, 8), (2, 5), (0, 2)]
GROUPS = [(14, 15), (12, 14), (10, 12), (8, 10), (6, 8), (4, 6), (2, 4), (1, 2), (0, 1)]
W1_WORD_LOADS = [(13, 15), (9, 13), (2, 9), (0, 2)]
W1_SCALE_LOADS = [(11, 15), (2, 11), (0, 2)]
W2_WORD_LOADS = [(9, 15), (2, 9), (0, 2)]
Y_BANK_EXPERTS = [(11, 15), (7, 11), (3, 7), (0, 3)]
TOKEN_CHUNKS = [(0, 2), (2, 3), (3, 4), (4, 5)]
VECTOR_WORD_GROUPS = (6, 7, 8)
Y_BANK = [[6, 7, 3, 0], [1, 2, 4, 5]]
SUM_BANK = [6, 7, 3, 3, 3]
BACK_BANK = [0, 1, 2, 4, 5]
SORT_CUTS = [[0, 2, 4], [0, 4], [0, 4], [0, 3, 4]]
GATE_LOADS = [(0, 3), (3, 5)]


def tile_moe_hot_mlp_relu_kernel(
    tc, x_words, x_scales, w1h_words, w1h_scales, w2h_words, w2h_scales,
    w1c_words, w1c_scales, w2c_words, w2c_scales, gate, offs, pos1, pos2, pos3,
    out_0, out_1, out_2,
):
    nc = tc.nc
    with ExitStack() as ctx:
        keep = ctx.enter_context(tc.tile_pool(name="keep", bufs=1))
        work = ctx.enter_context(tc.tile_pool(name="work", bufs=3))
        psum = ctx.enter_context(tc.psum_pool(name="psum", bufs=1))
        banks = [psum.tile([P, 512], F32, name="bank%d" % i) for i in range(8)]

        offs_t = keep.tile([P, S // 16], U16, name="offs_t")
        pos_t = [keep.tile([P, T // 16], U16, name="pos_t%d" % r) for r in range(TOP)]
        xw = keep.tile([P, T], I32, name="xw", align_bytes=64)
        xs = keep.tile([P, T], U8, name="xs", align_bytes=64)

        def scale_tile(name, lo, hi, width):
            t = keep.tile([P, hi - lo, width], U8, name="%s_%d" % (name, lo), align_bytes=64)
            engine = nc.vector if name == "s1" else nc.gpsimd
            engine.memset(t[:].rearrange("p e n -> p (e n)").bitcast(I32), 0)
            return t

        def load_scales(t, hot, cold, lo, hi, c0, c1):
            first = lo if lo < HOT else lo - HOT
            src = (hot if lo < HOT else cold).rearrange("e s b n -> (e s) b n").bitcast(I32)
            rows = src[first : first + hi - lo, :, c0 // 4 : c1 // 4].rearrange("e (q r) w -> r q e w", r=4)
            for r in range(4):
                nc.sync.dma_start(out=t[r:P:32].bitcast(I32), in_=rows[r])

        def load_words(name, hot, cold, lo, hi):
            if lo < HOT:
                src = hot.rearrange("e s p n d -> (e s) p (n d)").bitcast(I32)[lo:hi]
            else:
                src = cold.rearrange("e s p b -> (e s) p b").bitcast(I32)[lo - HOT : hi - HOT]
            shape = [P, hi - lo, 4 * src.shape[2]]
            t = keep.tile(shape, U8, name="%s_%d" % (name, lo), align_bytes=64)
            nc.sync.dma_start(out=t[:].bitcast(I32), in_=src.rearrange("e p w -> p e w"))
            return t

        nc.gpsimd.memset(xs[:].bitcast(I32), 0)
        warm = keep.tile([P, 16], F32, name="warm")
        nc.vector.memset(warm[:, 0:1], 0.0)
        s1 = {lo: scale_tile("s1", lo, hi, H) for lo, hi in W1_SCALE_LOADS}
        ident = keep.tile([P, P], F32, name="ident", align_bytes=64)
        make_identity(nc, ident[:])
        s2_hot = scale_tile("s2h", 0, HOT, N)
        s2_cold = [scale_tile("s2c%d" % a, HOT, E, N // 2) for a in range(2)]

        nc.scalar.activation(warm[:, 8:9], warm[:, 0:1], RELU)
        nc.sync.dma_start(offs_t[:], offs)
        x_rows = x_scales[0].rearrange("(q r) t -> r q t", r=4)
        for r in range(4):
            nc.sync.dma_start(out=xs[r:P:32].bitcast(I32), in_=x_rows[r].bitcast(I32))
        nc.sync.dma_start(out=xw[:], in_=x_words[0].rearrange("p t d -> p (t d)").bitcast(I32))
        w1 = {}
        w2 = {}
        for i in range(2):
            w1[W1_WORD_LOADS[i][0]] = load_words("w1", w1h_words, w1c_words, *W1_WORD_LOADS[i])
            lo, hi = W1_SCALE_LOADS[i]
            load_scales(s1[lo], w1h_scales, w1c_scales, lo, hi, 0, H)
        for lo, hi in W1_WORD_LOADS[2:]:
            w1[lo] = load_words("w1", w1h_words, w1c_words, lo, hi)
        w2[9] = load_words("w2", w2h_words, w2c_words, *W2_WORD_LOADS[0])
        load_scales(s1[0], w1h_scales, w1c_scales, 0, HOT, 0, H)
        w2[2] = load_words("w2", w2h_words, w2c_words, *W2_WORD_LOADS[1])
        load_scales(s2_hot, w2h_scales, w2c_scales, 0, HOT, 0, N)
        w2[0] = load_words("w2", w2h_words, w2c_words, *W2_WORD_LOADS[2])
        for r, src in enumerate((pos1, pos2, pos3)):
            nc.sync.dma_start(pos_t[r][:], src)
        gate_t = []
        for a, (b0, b1) in enumerate(GATE_LOADS):
            load_scales(s2_cold[a], w2h_scales, w2c_scales, HOT, E, a * N // 2, (a + 1) * N // 2)
            g = keep.tile([P, TOP, (b1 - b0) * P], F32, name="gate_t%d" % b0)
            nc.sync.dma_start(out=g[:], in_=gate.rearrange("r p t -> p r t")[:, :, b0 * P : b1 * P])
            gate_t.append(g)

        def second_scales(e, t):
            if e < HOT:
                return s2_hot[:, e, t * P : (t + 1) * P]
            return s2_cold[t // 2][:, e - HOT, t % 2 * P : (t % 2 + 1) * P]

        def held(tiles, loads, e):
            lo = [a for a, b in loads if a <= e < b][0]
            return tiles[lo][:, e - lo, :]

        def codes(words, e, c0, c1):
            if e < HOT:
                return words[:, 4 * c0 : 4 * c1].bitcast(FP8X4)
            return words[:, 2 * c0 : 2 * c1].bitcast(FP4X4)

        gathered = {}

        widest = max(hi - lo for lo, hi in GATHERS) * C
        gw_ring = [keep.tile([P, widest], U32, name="gw%d" % i, align_bytes=64) for i in range(3)]
        gs_ring = [keep.tile([P, widest], U8, name="gs%d" % i, align_bytes=64) for i in range(3)]

        def gather_tokens(i, lo, hi):
            n = (hi - lo) * C
            lst = offs_t[:, lo * C // 16 : hi * C // 16]
            gw = gw_ring[i % 3][:, 0:n]
            gs = gs_ring[i % 3][:, 0:n]
            nc.vector.tensor_copy(gw, xw[:].bitcast(U32).indirect(lst))
            nc.vector.tensor_copy(gs, xs[:].indirect(lst))
            for e in range(lo, hi):
                cols = slice((e - lo) * C, (e - lo + 1) * C)
                gathered[e] = (gw[:, cols], gs[:, cols])

        sorted_h = {}

        def first_product(e, bank):
            gw, gs = gathered[e]
            nc.tensor.matmul_mx(
                out=bank[:], lhsT=gw.bitcast(FP8X4), lhsT_scale=gs,
                rhs=codes(held(w1, W1_WORD_LOADS, e), e, 0, H), rhs_scale=held(s1, W1_SCALE_LOADS, e),
                start=True, stop=True,
            )
            hs = work.tile([P, H], BF16, name="hs", bufs=5, align_bytes=64)
            nc.scalar.activation(
                hs[:].rearrange("s (u m v) -> s u m v", u=2, v=2),
                bank[:].rearrange("s (m u v) -> s u m v", u=2, v=2), RELU,
            )
            sorted_h[e] = hs

        hq = {}

        def turn_and_quantise(g, lo, hi):
            n = hi - lo
            bank = banks[4 + g % 2][:, 0 : n * 2 * C].rearrange("p (e u s) -> p e u s", e=n, u=2)
            for e in range(lo, hi):
                words = sorted_h[e][:].bitcast(F32)
                for u in range(2):
                    nc.tensor.transpose(bank[:, e - lo, u, :], words[:, u * P : (u + 1) * P], ident[:])
            hb = work.tile([P, n * C * 4], BF16, name="hb", align_bytes=64)
            dst = hb[:].bitcast(F32).rearrange("p (e s u) -> p e s u", e=n, u=2)
            src = bank.rearrange("p e u s -> p e s u")
            if g in VECTOR_WORD_GROUPS:
                nc.vector.tensor_copy(dst, src)
            else:
                nc.scalar.copy(dst, src)
            qw = keep.tile([P, n * C], U32, name="qw%d" % lo, align_bytes=64)
            qs = keep.tile([P, n * C], U8, name="qs%d" % lo, align_bytes=64)
            nc.vector.quantize_mx(out=qw[:].bitcast(FP8X4), scales=qs[:], in_=hb[:])
            for e in range(lo, hi):
                cols = slice((e - lo) * C, (e - lo + 1) * C)
                hq[e] = (qw[:, cols], qs[:, cols])

        y = [keep.tile([P, S], F32, name="y%d" % t) for t in range(4)]

        def second_product(t, i, on_vector=False):
            lo, hi = Y_BANK_EXPERTS[i]
            bank = banks[Y_BANK[t % 2][i]]
            for e in reversed(range(lo, hi)):
                qw, qs = hq[e]
                nc.tensor.matmul_mx(
                    out=bank[:, (e - lo) * C : (e - lo + 1) * C],
                    lhsT=codes(held(w2, W2_WORD_LOADS, e), e, t * P, (t + 1) * P),
                    lhsT_scale=second_scales(e, t),
                    rhs=qw.bitcast(FP8X4), rhs_scale=qs, start=True, stop=True,
                )
            copy = nc.vector.tensor_copy if on_vector else nc.scalar.copy
            copy(y[t][:, lo * C : hi * C], bank[:, 0 : (hi - lo) * C])

        groups = GROUPS
        gathers = GATHERS
        gather_tokens(0, *gathers[0])
        for step in range(len(groups) + 1):
            if step + 1 < len(gathers):
                gather_tokens(step + 1, *gathers[step + 1])
            if step < len(groups):
                for e in reversed(range(*groups[step])):
                    first_product(e, banks[(E - 1 - e) % 4])
            if step >= 1:
                turn_and_quantise(step - 1, *groups[step - 1])
        for t in range(4):
            for i in range(len(Y_BANK_EXPERTS)):
                second_product(t, i, on_vector=(t == 0 and i % 2 == 1))

        ow = keep.tile([P, T], U32, name="ow", align_bytes=64)
        osc = keep.tile([P, T], U8, name="osc", align_bytes=64)
        out_rows = out_0.rearrange("(p j) t -> p j t", j=4)
        out_words = out_1[0].rearrange("p t d -> p (t d)").bitcast(I32)
        out_sc = out_2[0].rearrange("(q r) t -> r q t", r=4)
        wide = [[keep.tile([P, 2 * P], F32, name="g%d_%d" % (t, r)) for r in range(TOP)] for t in range(4)]
        spare = [keep.tile([P, P], F32, name="spare%d" % r) for r in range(TOP)]

        def products(ci, t):
            if ci == 0:
                return [g[:] for g in wide[t]]
            if (ci, t) == (1, 0):
                return [g[:] for g in spare]
            n = (t - 1) % 4
            return [g[:, n % 2 * P : (n % 2 + 1) * P] for g in wide[2 + n // 2]]

        def look_up(ci, t):
            b0, b1 = TOKEN_CHUNKS[ci]
            gi = [i for i, (a, b) in enumerate(GATE_LOADS) if a <= b0 < b][0]
            g0 = GATE_LOADS[gi][0]
            for r, g in enumerate(products(ci, t)):
                nc.vector.tensor_tensor(
                    g, y[t][:].indirect(pos_t[r][:, b0 * 8 : b1 * 8]),
                    gate_t[gi][:, r, (b0 - g0) * P : (b1 - g0) * P], MULT,
                )

        for ci, (b0, b1) in enumerate(TOKEN_CHUNKS):
            nb = b1 - b0
            last = ci == len(TOKEN_CHUNKS) - 1
            tok = slice(b0 * P, b1 * P)
            sums = [banks[SUM_BANK[b0 + b]][:].rearrange("k (t n) -> k t n", t=4) for b in range(nb)]
            turned = [keep.tile([P, 4, 4, 32], F32, name="turned%d" % (b0 + b)) for b in range(nb)]
            cuts = SORT_CUTS[ci]
            for t in range(4):
                if (ci, t) != (1, 0):
                    look_up(ci, t)
                if (ci, t) == (0, 0):
                    look_up(1, 0)
                parts = products(ci, t)
                for r in range(TOP):
                    for b in range(nb):
                        nc.tensor.matmul(
                            sums[b][:, t, :], parts[r][:, b * P : (b + 1) * P], ident[:],
                            start=(r == 0), stop=(r == TOP - 1), is_transpose=True,
                        )
                if t + 1 in cuts:
                    done = slice(cuts[cuts.index(t + 1) - 1], t + 1)
                    for b in range(nb):
                        nc.scalar.copy(
                            turned[b][:, :, done, :], sums[b][:, done, :].rearrange("k t (m j) -> k j t m", j=4)
                        )
            o32 = keep.tile([P, 4, nb * P], F32, name="o32_%d" % ci)
            for b in range(nb):
                back = banks[BACK_BANK[b0 + b]][:].rearrange("p (j k) -> p j k", j=4)
                for j in range(4):
                    nc.tensor.transpose(back[:, j, :], turned[b][:, j].rearrange("k t m -> k (t m)"), ident[:])
                ob = keep.tile([P, P * 4], BF16, name="ob%d" % (b0 + b), align_bytes=64)
                nc.scalar.copy(o32[:, :, b * P : (b + 1) * P], back)
                if last:
                    nc.vector.tensor_copy(ob[:].rearrange("p (k j) -> p k j", j=4), o32[:].rearrange("p j k -> p k j"))
                else:
                    nc.scalar.copy(ob[:].rearrange("p (k j) -> p k j", j=4), back.rearrange("p j k -> p k j"))
                cols = slice((b0 + b) * P, (b0 + b + 1) * P)
                nc.vector.quantize_mx(out=ow[:, cols].bitcast(FP8X4), scales=osc[:, cols], in_=ob[:])
            store = nc.scalar if last else nc.sync
            store.dma_start(out=out_rows[:, :, tok], in_=o32[:])
            nc.sync.dma_start(out=out_words[:, tok], in_=ow[:, tok].bitcast(I32))
        for r in range(4):
            store = nc.sync if r < 2 else nc.scalar
            store.dma_start(out=out_sc[r].bitcast(I32), in_=osc[r:P:32].bitcast(I32))
